import numpy as np
import ml_dtypes


def mxq(x, axis, fmt="e4m3"):
    dtype, down = {"e4m3": (ml_dtypes.float8_e4m3fn, 7), "e5m2": (ml_dtypes.float8_e5m2, 14)}[fmt]
    v = np.moveaxis(np.asarray(x, np.float32).astype(ml_dtypes.bfloat16).astype(np.float64), axis, -1)
    blocks = v.reshape(v.shape[:-1] + (-1, 32))
    amax = np.abs(blocks).max(-1, keepdims=True)
    byte = np.maximum(np.where(amax > 0, np.frexp(amax)[1] - 1 + 127, 0) - down, 1)
    scale = np.exp2(byte - 127.0)
    codes = (blocks / scale).astype(np.float32).astype(dtype).astype(np.float64)
    return np.moveaxis((codes * scale).reshape(v.shape), -1, axis)


WIDE = False


def mx_kscale(k):
    if not WIDE:
        return np.ones(k)
    levels = np.array([10, -10, 5, -5, 0])
    if k % 512:
        return np.exp2(np.random.permutation(np.resize(levels, k // 32))).repeat(32)
    a = np.empty((k // 512, 16))
    for p in range(k // 512):
        a[p, :8] = np.random.permutation(np.resize(levels, 8))
        for g in range(8):
            far = levels[np.abs(levels - a[p, g]) >= 10]
            a[p, g + 8] = far[np.random.randint(len(far))]
    return np.exp2(a.ravel()).repeat(32)


def f64(x):
    return np.asarray(x).astype(np.float64)


def striped(idx):
    return np.tile(idx.reshape(-1, 16).T, (8, 1)).astype(np.uint16)


def unstriped(offs):
    return offs[:16].T.reshape(-1).astype(np.int64)


def pack_weight(w):
    k, n = w.shape
    w = f64(np.asarray(w, np.float32).astype(ml_dtypes.bfloat16)).reshape(k // 32, 32, n)
    amax = np.abs(w).max(1)
    byte = np.clip(np.where(amax > 0, np.frexp(amax)[1] - 1 + 127 - 7, 1), 1, 254)
    scaled = (w * np.exp2(127.0 - byte)[:, None, :]).reshape(k, n).astype(np.float32)
    words = np.ascontiguousarray(scaled.reshape(k // 512, 128, 4, n).transpose(0, 1, 3, 2)).astype(ml_dtypes.float8_e4m3fn).view(np.uint8)
    return words, np.ascontiguousarray(byte.astype(np.uint8).reshape(k // 512, 16, n))


def unpack_weight(words, scales):
    g, p, n, _ = words.shape
    vals = np.ascontiguousarray(words).view(ml_dtypes.float8_e4m3fn).astype(np.float64) * np.repeat(np.exp2(scales.astype(np.float64) - 127.0), 8, axis=1)[..., None]
    return vals.transpose(0, 1, 3, 2).reshape(g * 512, n)


K, T, E, C, N = 512, 1024, 16, 128, 256


def by_expert(wq, xq):
    return np.concatenate([wq[e].T @ xq[:, e * C:(e + 1) * C] for e in range(E)], axis=1)


def setup_inputs():
    n = np.random.standard_normal
    s = mx_kscale(K)[:, None]
    first = np.random.permutation(np.repeat(np.arange(E), T // E))
    second = (first + 1 + np.random.permutation(np.repeat(np.arange(E - 1), -(-T // (E - 1)))[:T])) % E
    while np.bincount(second, minlength=E).max() != T // E:
        load = np.bincount(second, minlength=E); hi, lo = int(load.argmax()), int(load.argmin())
        t = np.flatnonzero((second == hi) & (first != lo))[0]; second[t] = lo
    slot_token = np.empty(E * C, np.int64); pos = np.empty((2, T), np.int64); fill = np.zeros(E, np.int64)
    place = np.stack([np.random.permutation(C) for _ in range(E)])
    for r, deal in enumerate((first, second)):
        for t in np.random.permutation(T):
            e = deal[t]; j = e * C + place[e, fill[e]]; fill[e] += 1; slot_token[j] = t; pos[r, t] = j
    g = np.random.uniform(0.2, 0.8, T)
    packed = [pack_weight(m) for m in n((E, K, N)) / np.sqrt(K) / s[None]]
    return {
        "xT": (n((K, T)) * s).astype(np.float32),
        "w_words": np.stack([m[0] for m in packed]),
        "w_scales": np.stack([m[1] for m in packed]),
        "b": (0.3 * n((N, E))).astype(np.float32),
        "gate": np.stack([np.tile(g, (N, 1)), np.tile(1.0 - g, (N, 1))]).astype(np.float32),
        "offs": striped(slot_token),
        "pos1": striped(pos[0]),
        "pos2": striped(pos[1]),
    }


def reference(xT, w_words, w_scales, b, gate, offs, pos1, pos2):
    idx = unstriped(offs)
    xq = mxq(f64(xT)[:, idx], 0, "e4m3")
    w = np.stack([unpack_weight(w_words[e], w_scales[e]) for e in range(E)])
    y = by_expert(w, xq)
    y = y + np.repeat(f64(b), C, axis=1)
    return f64(gate[0]) * y[:, unstriped(pos1)] + f64(gate[1]) * y[:, unstriped(pos2)]

@@ -1,0 +1,124 @@
+from contextlib import ExitStack
+
+import concourse.mybir as mybir
+
+K, T, E, C, N = 512, 1024, 16, 128, 256
+SLOTS = E * C
+
+F32 = mybir.dt.float32
+BF16 = mybir.dt.bfloat16
+I32 = mybir.dt.int32
+U32 = mybir.dt.uint32
+U16 = mybir.dt.uint16
+U8 = mybir.dt.uint8
+FP8X4 = mybir.dt.float8_e4m3fn_x4
+MULT = mybir.AluOpType.mult
+ADD = mybir.AluOpType.add
+IDENTITY = mybir.ActivationFunctionType.Identity
+
+P = 128
+PACK = 4
+HALVES = N // P
+
+FLOPS = 2 * SLOTS * K * N
+BYTES = 4 * K * T + E * K * N + E * (K // 32) * N + 4 * N * E + 2 * 4 * T + 2 * 128 * 256 + 4 * N * T
+
+LOADS = [(0, 256, 128), (256, 256, 128), (512, 256, 128), (768, 256, 176)]
+GATHERS = [512, 512, 512, 256, 128, 128]
+COMBINES = [[512, 512], [512, 256, 128, 128]]
+W_LOAD = 4
+
+
+def tile_routed_moe_kernel(tc, xT, w_words, w_scales, b, gate, offs, pos1, pos2, out):
+    nc = tc.nc
+    with ExitStack() as ctx:
+        keep = ctx.enter_context(tc.tile_pool(name="keep", bufs=1))
+        psum = ctx.enter_context(tc.psum_pool(name="psum", bufs=8))
+
+        offs_sb = keep.tile([P, SLOTS // 16], U16, name="offs_sb")
+        pos_sb = [keep.tile([P, T // 16], U16, name=f"pos{r}_sb") for r in range(2)]
+
+        words = keep.tile([P, T], U32, align_bytes=64, name="words")
+        scales = keep.tile([P, T], U8, align_bytes=64, name="scales")
+        slot_words = keep.tile([P, SLOTS], U32, align_bytes=64, name="slot_words")
+        slot_scales = keep.tile([P, SLOTS], U8, align_bytes=64, name="slot_scales")
+        w_sb = keep.tile([P, E, N], U32, align_bytes=64, name="w_sb")
+        ws_sb = keep.tile([P, E, N], U8, align_bytes=64, name="ws_sb")
+        b_sb = keep.tile([P, HALVES, E], F32, name="b_sb")
+        gate_sb = keep.tile([P, 2, T], F32, name="gate_sb")
+        sums = [keep.tile([P, SLOTS], F32, name=f"sums{h}") for h in range(HALVES)]
+
+        nc.gpsimd.memset(scales[:], 0)
+        nc.gpsimd.memset(ws_sb[:].rearrange("p e n -> p (e n)").bitcast(I32), 0)
+
+        raws = []
+        for t0, n, _ in LOADS:
+            raw = keep.tile([P, PACK, n], F32, name=f"raw{t0}")
+            nc.sync.dma_start(raw[:], xT[:, t0 : t0 + n].rearrange("(p j) n -> p j n", j=PACK))
+            raws.append(raw)
+        nc.sync.dma_start(offs_sb[:], offs)
+        for q in range(4):
+            nc.sync.dma_start(
+                ws_sb[32 * q : 32 * q + 4, :, :].bitcast(I32),
+                w_scales[:, 0, 4 * q : 4 * q + 4, :].rearrange("e r n -> r e n").bitcast(I32),
+            )
+        for e0 in range(0, E, W_LOAD):
+            nc.sync.dma_start(
+                w_sb[:, e0 : e0 + W_LOAD, :].bitcast(I32),
+                w_words[e0 : e0 + W_LOAD, 0].rearrange("e p n r -> p e (n r)").bitcast(I32),
+            )
+            if e0 == 0:
+                nc.sync.dma_start(b_sb[:], b.rearrange("(h p) e -> p h e", p=P))
+        nc.sync.dma_start(pos_sb[0][:], pos1)
+        nc.sync.dma_start(pos_sb[1][:], pos2)
+        nc.sync.dma_start(gate_sb[:], gate[:, 0:P, :].rearrange("r p t -> p r t"))
+
+        for (t0, n, cut), raw in zip(LOADS, raws):
+            grouped = keep.tile([P, n, PACK], BF16, align_bytes=64, name=f"grouped{t0}")
+            src = raw[:].rearrange("p j n -> p n j")
+            nc.scalar.copy(grouped[:, cut:n, :], src[:, cut:n, :])
+            nc.vector.tensor_copy(grouped[:, 0:cut, :], src[:, 0:cut, :])
+            nc.vector.quantize_mx(
+                out=words[:, t0 : t0 + n].bitcast(FP8X4),
+                scales=scales[:, t0 : t0 + n],
+                in_=grouped[:].rearrange("p n j -> p (n j)"),
+            )
+
+        s0 = 0
+        for n in GATHERS:
+            cols = slice(s0, s0 + n)
+            picks = offs_sb[:, s0 // 16 : (s0 + n) // 16]
+            nc.vector.tensor_copy(slot_words[:, cols], words[:].indirect(picks))
+            nc.vector.tensor_copy(slot_scales[:, cols], scales[:].indirect(picks))
+            for e in range(s0 // C, (s0 + n) // C):
+                mine = slice(e * C, (e + 1) * C)
+                acc = psum.tile([P, HALVES, C], F32, name="acc")
+                for h in range(HALVES):
+                    nc.tensor.matmul_mx(
+                        out=acc[:, h, :],
+                        lhsT=w_sb[:, e, h * P : (h + 1) * P].bitcast(FP8X4),
+                        lhsT_scale=ws_sb[:, e, h * P : (h + 1) * P],
+                        rhs=slot_words[:, mine].bitcast(FP8X4),
+                        rhs_scale=slot_scales[:, mine],
+                        start=True,
+                        stop=True,
+                    )
+                for h in range(HALVES):
+                    nc.scalar.activation(sums[h][:, mine], acc[:, h, :], IDENTITY, bias=b_sb[:, h, e : e + 1])
+            s0 += n
+
+        for h in range(HALVES):
+            t0 = 0
+            for n in COMBINES[h]:
+                cols = slice(t0, t0 + n)
+                parts = []
+                for r in range(2):
+                    part = keep.tile([P, n], F32, name=f"part{h}_{t0}_{r}")
+                    nc.vector.tensor_tensor(
+                        part[:], sums[h][:].indirect(pos_sb[r][:, t0 // 16 : (t0 + n) // 16]), gate_sb[:, r, cols], MULT
+                    )
+                    parts.append(part)
+                total = keep.tile([P, n], F32, name=f"total{h}_{t0}")
+                nc.vector.tensor_tensor(total[:], parts[0][:], parts[1][:], ADD)
+                nc.sync.dma_start(out[h * P : (h + 1) * P, cols], total[:])
+                t0 += n

@@ -1,6 +1,7 @@
 from contextlib import ExitStack
 
 import concourse.mybir as mybir
+from concourse.masks import make_identity
 
 K, T, E, C, N = 512, 1024, 16, 128, 256
 SLOTS = E * C
@@ -23,9 +24,11 @@ HALVES = N // P
 FLOPS = 2 * SLOTS * K * N
 BYTES = 4 * K * T + E * K * N + E * (K // 32) * N + 4 * N * E + 2 * 4 * T + 2 * 128 * 256 + 4 * N * T
 
-LOADS = [(0, 256, 128), (256, 256, 128), (512, 256, 128), (768, 256, 176)]
-GATHERS = [512, 512, 512, 256, 128, 128]
-COMBINES = [[512, 512], [512, 256, 128, 128]]
+LOADS = [(0, 256, 88), (256, 256, 104), (512, 256, 128), (768, 256, 160)]
+GATHERS = [768, 768, 384, 128]
+COMBINES = [[(800, True), (224, False)], [(768, False), (256, False)]]
+V_EVACUATES = [15]
+BANKS = 4
 W_LOAD = 4
 
 
@@ -33,7 +36,7 @@ def tile_routed_moe_kernel(tc, xT, w_words, w_scales, b, gate, offs, pos1, pos2,
     nc = tc.nc
     with ExitStack() as ctx:
         keep = ctx.enter_context(tc.tile_pool(name="keep", bufs=1))
-        psum = ctx.enter_context(tc.psum_pool(name="psum", bufs=8))
+        psum = ctx.enter_context(tc.psum_pool(name="psum", bufs=1))
 
         offs_sb = keep.tile([P, SLOTS // 16], U16, name="offs_sb")
         pos_sb = [keep.tile([P, T // 16], U16, name=f"pos{r}_sb") for r in range(2)]
@@ -48,8 +51,10 @@ def tile_routed_moe_kernel(tc, xT, w_words, w_scales, b, gate, offs, pos1, pos2,
         gate_sb = keep.tile([P, 2, T], F32, name="gate_sb")
         sums = [keep.tile([P, SLOTS], F32, name=f"sums{h}") for h in range(HALVES)]
 
-        nc.gpsimd.memset(scales[:], 0)
+        ident = keep.tile([P, P], F32, name="ident")
         nc.gpsimd.memset(ws_sb[:].rearrange("p e n -> p (e n)").bitcast(I32), 0)
+        nc.gpsimd.memset(scales[:], 0)
+        make_identity(nc, ident[:])
 
         raws = []
         for t0, n, _ in LOADS:
@@ -84,6 +89,18 @@ def tile_routed_moe_kernel(tc, xT, w_words, w_scales, b, gate, offs, pos1, pos2,
                 in_=grouped[:].rearrange("p n j -> p (n j)"),
             )
 
+        acc = [[psum.tile([P, E // BANKS, C], F32, name=f"acc{h}_{i}") for i in range(BANKS)] for h in range(HALVES)]
+
+        def evacuate(h, e):
+            if h == 0 and e in V_EVACUATES:
+                nc.vector.tensor_scalar_add(
+                    sums[h][:, e * C : (e + 1) * C], acc[h][e % BANKS][:, e // BANKS, :], b_sb[:, h, e : e + 1]
+                )
+                return
+            nc.scalar.activation(
+                sums[h][:, e * C : (e + 1) * C], acc[h][e % BANKS][:, e // BANKS, :], IDENTITY, bias=b_sb[:, h, e : e + 1]
+            )
+
         s0 = 0
         for n in GATHERS:
             cols = slice(s0, s0 + n)
@@ -92,10 +109,9 @@ def tile_routed_moe_kernel(tc, xT, w_words, w_scales, b, gate, offs, pos1, pos2,
             nc.vector.tensor_copy(slot_scales[:, cols], scales[:].indirect(picks))
             for e in range(s0 // C, (s0 + n) // C):
                 mine = slice(e * C, (e + 1) * C)
-                acc = psum.tile([P, HALVES, C], F32, name="acc")
                 for h in range(HALVES):
                     nc.tensor.matmul_mx(
-                        out=acc[:, h, :],
+                        out=acc[h][e % BANKS][:, e // BANKS, :],
                         lhsT=w_sb[:, e, h * P : (h + 1) * P].bitcast(FP8X4),
                         lhsT_scale=ws_sb[:, e, h * P : (h + 1) * P],
                         rhs=slot_words[:, mine].bitcast(FP8X4),
@@ -103,22 +119,33 @@ def tile_routed_moe_kernel(tc, xT, w_words, w_scales, b, gate, offs, pos1, pos2,
                         start=True,
                         stop=True,
                     )
-                for h in range(HALVES):
-                    nc.scalar.activation(sums[h][:, mine], acc[:, h, :], IDENTITY, bias=b_sb[:, h, e : e + 1])
+                evacuate(0, e)
             s0 += n
 
         for h in range(HALVES):
             t0 = 0
-            for n in COMBINES[h]:
-                cols = slice(t0, t0 + n)
+            for n, on_tensor in COMBINES[h]:
                 parts = []
                 for r in range(2):
                     part = keep.tile([P, n], F32, name=f"part{h}_{t0}_{r}")
                     nc.vector.tensor_tensor(
-                        part[:], sums[h][:].indirect(pos_sb[r][:, t0 // 16 : (t0 + n) // 16]), gate_sb[:, r, cols], MULT
+                        part[:],
+                        sums[h][:].indirect(pos_sb[r][:, t0 // 16 : (t0 + n) // 16]),
+                        gate_sb[:, r, t0 : t0 + n],
+                        MULT,
                     )
                     parts.append(part)
                 total = keep.tile([P, n], F32, name=f"total{h}_{t0}")
-                nc.vector.tensor_tensor(total[:], parts[0][:], parts[1][:], ADD)
-                nc.sync.dma_start(out[h * P : (h + 1) * P, cols], total[:])
+                if on_tensor:
+                    for e in range(E):
+                        evacuate(1, e)
+                    for c0 in range(0, n, 400):
+                        cols = slice(c0, c0 + 400)
+                        both = psum.tile([P, 400], F32, name=f"acc0_{c0 // 400}")
+                        nc.tensor.matmul(both[:], ident[:], parts[0][:, cols], start=True, stop=False)
+                        nc.tensor.matmul(both[:], ident[:], parts[1][:, cols], start=False, stop=True)
+                        nc.scalar.copy(total[:, cols], both[:])
+                else:
+                    nc.vector.tensor_tensor(total[:], parts[0][:], parts[1][:], ADD)
+                nc.sync.dma_start(out[h * P : (h + 1) * P, t0 : t0 + n], total[:])
                 t0 += n

@@ -24,9 +24,9 @@ HALVES = N // P
 FLOPS = 2 * SLOTS * K * N
 BYTES = 4 * K * T + E * K * N + E * (K // 32) * N + 4 * N * E + 2 * 4 * T + 2 * 128 * 256 + 4 * N * T
 
-LOADS = [(0, 256, 88), (256, 256, 104), (512, 256, 128), (768, 256, 160)]
+LOADS = [(0, 256, 96), (256, 256, 112), (512, 256, 136), (768, 256, 168)]
 GATHERS = [768, 768, 384, 128]
-COMBINES = [[(800, True), (224, False)], [(768, False), (256, False)]]
+COMBINES = [(0, 0, 800), (0, 800, 224), (1, 0, 640), (1, 640, 256), (1, 896, 128)]
 V_EVACUATES = [15]
 BANKS = 4
 W_LOAD = 4
@@ -122,30 +122,41 @@ def tile_routed_moe_kernel(tc, xT, w_words, w_scales, b, gate, offs, pos1, pos2,
                 evacuate(0, e)
             s0 += n
 
-        for h in range(HALVES):
-            t0 = 0
-            for n, on_tensor in COMBINES[h]:
-                parts = []
-                for r in range(2):
-                    part = keep.tile([P, n], F32, name=f"part{h}_{t0}_{r}")
-                    nc.vector.tensor_tensor(
-                        part[:],
-                        sums[h][:].indirect(pos_sb[r][:, t0 // 16 : (t0 + n) // 16]),
-                        gate_sb[:, r, t0 : t0 + n],
-                        MULT,
-                    )
-                    parts.append(part)
-                total = keep.tile([P, n], F32, name=f"total{h}_{t0}")
-                if on_tensor:
-                    for e in range(E):
-                        evacuate(1, e)
-                    for c0 in range(0, n, 400):
-                        cols = slice(c0, c0 + 400)
-                        both = psum.tile([P, 400], F32, name=f"acc0_{c0 // 400}")
-                        nc.tensor.matmul(both[:], ident[:], parts[0][:, cols], start=True, stop=False)
-                        nc.tensor.matmul(both[:], ident[:], parts[1][:, cols], start=False, stop=True)
-                        nc.scalar.copy(total[:, cols], both[:])
-                else:
-                    nc.vector.tensor_tensor(total[:], parts[0][:], parts[1][:], ADD)
-                nc.sync.dma_start(out[h * P : (h + 1) * P, t0 : t0 + n], total[:])
-                t0 += n
+        def fetch(h, r, t0, n):
+            part = keep.tile([P, n], F32, name=f"part{h}_{t0}_{r}")
+            nc.vector.tensor_tensor(
+                part[:],
+                sums[h][:].indirect(pos_sb[r][:, t0 // 16 : (t0 + n) // 16]),
+                gate_sb[:, r, t0 : t0 + n],
+                MULT,
+            )
+            return part
+
+        def add(h, t0, n, parts, on_tensor):
+            total = keep.tile([P, n], F32, name=f"total{h}_{t0}")
+            if on_tensor:
+                for c0 in range(0, n, 400):
+                    cols = slice(c0, c0 + 400)
+                    both = psum.tile([P, 400], F32, name=f"acc0_{c0 // 400}")
+                    nc.tensor.matmul(both[:], ident[:], parts[0][:, cols], start=True, stop=False)
+                    nc.tensor.matmul(both[:], ident[:], parts[1][:, cols], start=False, stop=True)
+                    nc.scalar.copy(total[:, cols], both[:])
+            else:
+                nc.vector.tensor_tensor(total[:], parts[0][:], parts[1][:], ADD)
+            nc.sync.dma_start(out[h * P : (h + 1) * P, t0 : t0 + n], total[:])
+
+        waiting = []
+        for h, t0, n in COMBINES:
+            first = fetch(h, 0, t0, n)
+            if waiting and t0 + n < T:
+                add(*waiting.pop())
+            second = fetch(h, 1, t0, n)
+            if waiting:
+                add(*waiting.pop())
+            if t0 == 0 and h == 0:
+                for e in range(E):
+                    evacuate(1, e)
+                add(h, t0, n, (first, second), True)
+            else:
+                waiting.append((h, t0, n, (first, second), False))
+        add(*waiting.pop())

from contextlib import ExitStack

import concourse.mybir as mybir
from concourse.masks import make_identity

K, T, E, C, N = 512, 1024, 16, 128, 256
SLOTS = E * C

F32 = mybir.dt.float32
BF16 = mybir.dt.bfloat16
I32 = mybir.dt.int32
U32 = mybir.dt.uint32
U16 = mybir.dt.uint16
U8 = mybir.dt.uint8
FP8X4 = mybir.dt.float8_e4m3fn_x4
MULT = mybir.AluOpType.mult
ADD = mybir.AluOpType.add
IDENTITY = mybir.ActivationFunctionType.Identity

P = 128
PACK = 4
HALVES = N // P

FLOPS = 2 * SLOTS * K * N
BYTES = 4 * K * T + E * K * N + E * (K // 32) * N + 4 * N * E + 2 * 4 * T + 2 * 128 * 256 + 4 * N * T

LOADS = [(0, 256, 96), (256, 256, 112), (512, 256, 136), (768, 256, 168)]
GATHERS = [768, 768, 384, 128]
COMBINES = [(0, 0, 800), (0, 800, 224), (1, 0, 640), (1, 640, 256), (1, 896, 128)]
V_EVACUATES = [15]
BANKS = 4
W_LOAD = 4


def tile_routed_moe_kernel(tc, xT, w_words, w_scales, b, gate, offs, pos1, pos2, out):
    nc = tc.nc
    with ExitStack() as ctx:
        keep = ctx.enter_context(tc.tile_pool(name="keep", bufs=1))
        psum = ctx.enter_context(tc.psum_pool(name="psum", bufs=1))

        offs_sb = keep.tile([P, SLOTS // 16], U16, name="offs_sb")
        pos_sb = [keep.tile([P, T // 16], U16, name=f"pos{r}_sb") for r in range(2)]

        words = keep.tile([P, T], U32, align_bytes=64, name="words")
        scales = keep.tile([P, T], U8, align_bytes=64, name="scales")
        slot_words = keep.tile([P, SLOTS], U32, align_bytes=64, name="slot_words")
        slot_scales = keep.tile([P, SLOTS], U8, align_bytes=64, name="slot_scales")
        w_sb = keep.tile([P, E, N], U32, align_bytes=64, name="w_sb")
        ws_sb = keep.tile([P, E, N], U8, align_bytes=64, name="ws_sb")
        b_sb = keep.tile([P, HALVES, E], F32, name="b_sb")
        gate_sb = keep.tile([P, 2, T], F32, name="gate_sb")
        sums = [keep.tile([P, SLOTS], F32, name=f"sums{h}") for h in range(HALVES)]

        ident = keep.tile([P, P], F32, name="ident")
        nc.gpsimd.memset(ws_sb[:].rearrange("p e n -> p (e n)").bitcast(I32), 0)
        nc.gpsimd.memset(scales[:], 0)
        make_identity(nc, ident[:])

        raws = []
        for t0, n, _ in LOADS:
            raw = keep.tile([P, PACK, n], F32, name=f"raw{t0}")
            nc.sync.dma_start(raw[:], xT[:, t0 : t0 + n].rearrange("(p j) n -> p j n", j=PACK))
            raws.append(raw)
        nc.sync.dma_start(offs_sb[:], offs)
        for q in range(4):
            nc.sync.dma_start(
                ws_sb[32 * q : 32 * q + 4, :, :].bitcast(I32),
                w_scales[:, 0, 4 * q : 4 * q + 4, :].rearrange("e r n -> r e n").bitcast(I32),
            )
        for e0 in range(0, E, W_LOAD):
            nc.sync.dma_start(
                w_sb[:, e0 : e0 + W_LOAD, :].bitcast(I32),
                w_words[e0 : e0 + W_LOAD, 0].rearrange("e p n r -> p e (n r)").bitcast(I32),
            )
            if e0 == 0:
                nc.sync.dma_start(b_sb[:], b.rearrange("(h p) e -> p h e", p=P))
        nc.sync.dma_start(pos_sb[0][:], pos1)
        nc.sync.dma_start(pos_sb[1][:], pos2)
        nc.sync.dma_start(gate_sb[:], gate[:, 0:P, :].rearrange("r p t -> p r t"))

        for (t0, n, cut), raw in zip(LOADS, raws):
            grouped = keep.tile([P, n, PACK], BF16, align_bytes=64, name=f"grouped{t0}")
            src = raw[:].rearrange("p j n -> p n j")
            nc.scalar.copy(grouped[:, cut:n, :], src[:, cut:n, :])
            nc.vector.tensor_copy(grouped[:, 0:cut, :], src[:, 0:cut, :])
            nc.vector.quantize_mx(
                out=words[:, t0 : t0 + n].bitcast(FP8X4),
                scales=scales[:, t0 : t0 + n],
                in_=grouped[:].rearrange("p n j -> p (n j)"),
            )

        acc = [[psum.tile([P, E // BANKS, C], F32, name=f"acc{h}_{i}") for i in range(BANKS)] for h in range(HALVES)]

        def evacuate(h, e):
            if h == 0 and e in V_EVACUATES:
                nc.vector.tensor_scalar_add(
                    sums[h][:, e * C : (e + 1) * C], acc[h][e % BANKS][:, e // BANKS, :], b_sb[:, h, e : e + 1]
                )
                return
            nc.scalar.activation(
                sums[h][:, e * C : (e + 1) * C], acc[h][e % BANKS][:, e // BANKS, :], IDENTITY, bias=b_sb[:, h, e : e + 1]
            )

        s0 = 0
        for n in GATHERS:
            cols = slice(s0, s0 + n)
            picks = offs_sb[:, s0 // 16 : (s0 + n) // 16]
            nc.vector.tensor_copy(slot_words[:, cols], words[:].indirect(picks))
            nc.vector.tensor_copy(slot_scales[:, cols], scales[:].indirect(picks))
            for e in range(s0 // C, (s0 + n) // C):
                mine = slice(e * C, (e + 1) * C)
                for h in range(HALVES):
                    nc.tensor.matmul_mx(
                        out=acc[h][e % BANKS][:, e // BANKS, :],
                        lhsT=w_sb[:, e, h * P : (h + 1) * P].bitcast(FP8X4),
                        lhsT_scale=ws_sb[:, e, h * P : (h + 1) * P],
                        rhs=slot_words[:, mine].bitcast(FP8X4),
                        rhs_scale=slot_scales[:, mine],
                        start=True,
                        stop=True,
                    )
                evacuate(0, e)
            s0 += n

        def fetch(h, r, t0, n):
            part = keep.tile([P, n], F32, name=f"part{h}_{t0}_{r}")
            nc.vector.tensor_tensor(
                part[:],
                sums[h][:].indirect(pos_sb[r][:, t0 // 16 : (t0 + n) // 16]),
                gate_sb[:, r, t0 : t0 + n],
                MULT,
            )
            return part

        def add(h, t0, n, parts, on_tensor):
            total = keep.tile([P, n], F32, name=f"total{h}_{t0}")
            if on_tensor:
                for c0 in range(0, n, 400):
                    cols = slice(c0, c0 + 400)
                    both = psum.tile([P, 400], F32, name=f"acc0_{c0 // 400}")
                    nc.tensor.matmul(both[:], ident[:], parts[0][:, cols], start=True, stop=False)
                    nc.tensor.matmul(both[:], ident[:], parts[1][:, cols], start=False, stop=True)
                    nc.scalar.copy(total[:, cols], both[:])
            else:
                nc.vector.tensor_tensor(total[:], parts[0][:], parts[1][:], ADD)
            nc.sync.dma_start(out[h * P : (h + 1) * P, t0 : t0 + n], total[:])

        waiting = []
        for h, t0, n in COMBINES:
            first = fetch(h, 0, t0, n)
            if waiting and t0 + n < T:
                add(*waiting.pop())
            second = fetch(h, 1, t0, n)
            if waiting:
                add(*waiting.pop())
            if t0 == 0 and h == 0:
                for e in range(E):
                    evacuate(1, e)
                add(h, t0, n, (first, second), True)
            else:
                waiting.append((h, t0, n, (first, second), False))
        add(*waiting.pop())
